import numpy as np, ml_dtypes
CORES = [12,28,60,100,156,228]
N = 6
R, TK = 64, 128
def setup_inputs(rng):
    v = (rng.standard_normal((N, 128, R), dtype=np.float32) / np.float32(np.sqrt(128 * N))).astype(ml_dtypes.bfloat16)
    return {"x": rng.standard_normal((N, 128, TK), dtype=np.float32).astype(ml_dtypes.bfloat16), "v": v, "vt": v.transpose(0, 2, 1).copy()}
def setup_inputs_big(rng):
    d = setup_inputs(rng)
    for k in ("x",): d[k] = (d[k].astype(np.float32) * 1048576.0).astype(d[k].dtype)
    return d
def setup_inputs_small(rng):
    d = setup_inputs(rng)
    for k in ("x",): d[k] = (d[k].astype(np.float32) * (1 / 1048576.0)).astype(d[k].dtype)
    return d
def setup_inputs_apart(rng):
    d = setup_inputs(rng)
    f = (10.0 ** rng.permutation(np.linspace(-1.5, 1.5, N))).astype(np.float32).reshape(N, 1, 1)
    for k in ("x",): d[k] = (d[k].astype(np.float32) * f).astype(d[k].dtype)
    return d
def reference(x, v, vt):
    X, V, VT = x.astype(np.float64), v.astype(np.float64), vt.astype(np.float64)
    t = sum(V[j].T @ X[j] for j in range(N))
    return {"y": np.stack([X[r] - 2.0 * (VT[r].T @ t) for r in range(N)]).astype(ml_dtypes.bfloat16)}

from concourse.bass import DstId, RemoteDMATransfer
from concourse.mybir import AluOpType

N = 6
HALF = 64
PER_RELAY = 2
K_HAND = 4
K_FAR = 4
K_NEAR = 8

SCRATCH = {
    "xs": ("sbuf", [128, 128], "bfloat16"),
    "vs": ("sbuf", [128, HALF], "bfloat16"),
    "vtt": ("sbuf", [128, 128], "bfloat16"),
    "vt2": ("sbuf", [128, 128], "bfloat16"),
    "ps": ("sbuf", [128, HALF], "bfloat16"),
    "land": ("sbuf", [128, N * HALF], "bfloat16"),
    "ys": ("sbuf", [128, 128], "bfloat16"),
    "pp": ("psum", [128, 512], "float32"),
    "accl": ("psum", [128, 512], "float32"),
    "accr": ("psum", [128, 512], "float32"),
}
SEMAPHORES = ["ld", "lvt", "mm", "pc", "nv", "fl", "fr", "yd", "st", "ls", "h"] + ["a%d" % j for j in range(N)]


def _engines(mask, n, skip=0):
    bits = [b for b in range(mask.bit_length()) if (mask >> b) & 1]
    m = 0
    for b in bits[skip:skip + n]:
        m |= 1 << b
    return m


def _plan(T, topo):
    cores = list(T.cores)
    near, relays = {}, {}
    for i, c in enumerate(cores):
        near[i] = [j for j, d in enumerate(cores) if j != i and topo.may_write(c, d)]
        far = [j for j, d in enumerate(cores) if j != i and not topo.may_write(c, d)]
        span = topo.CORES_PER_CHIP
        cand = [h for h in range(max(0, c - span + 1), c + span)
                if h != c and topo.host(h) == topo.host(c) and topo.chip(h) == topo.chip(c)
                and T.rank_of(h) is None and all(topo.may_write(h, cores[j]) for j in far)]
        cand.sort(key=lambda h: (topo.die(h) != topo.die(c), h))
        groups = [far[k:k + PER_RELAY] for k in range(0, len(far), PER_RELAY)]
        relays[i] = [(cand[k], grp) for k, grp in enumerate(groups)]
    return cores, near, relays


def _dst(topo, d, src):
    rid, pid = topo.addr(d, src)
    return DstId(rid=rid, pnc=pid)


def _relay_program(g, core, T, topo, cores, src, grp):
    sem = T.sem
    slot = T.land[:, src * HALF:(src + 1) * HALF]
    g.wait_ge(sem.h, K_HAND)
    g.remote_dma_fused(
        [RemoteDMATransfer(dst_ids=[_dst(topo, cores[j], core)],
                           dma_engine_mask=_engines(topo.mask(core, cores[j]), K_FAR, k * K_FAR),
                           remote_sem=sem["a%d" % src], src=T.ps[:], dst=slot)
         for k, j in enumerate(grp)],
        local_sem=sem.ls)
    g.wait_ge(sem.ls, K_FAR * len(grp))


def rank_program(g, core, T, topo):
    cores, near, relays = _plan(T, topo)
    rank = T.rank_of(core)
    if rank is None:
        for i in range(len(cores)):
            for h, grp in relays[i]:
                if h == core:
                    _relay_program(g, core, T, topo, cores, i, grp)
        return
    sem = T.sem
    top, bot = slice(0, HALF), slice(HALF, 2 * HALF)

    g.sync.dma_start(T.xs[:], T.x[:]).then_inc(sem.ld, 16)
    g.scalar.dma_start(T.vs[:], T.v[:]).then_inc(sem.ld, 16)
    g.sync.dma_start(T.vtt[top, :], T.vt[:]).then_inc(sem.lvt, 16)
    g.scalar.dma_start(T.vtt[bot, :], T.vt[:]).then_inc(sem.lvt, 16)

    g.tensor.wait_ge(sem.ld, 32)
    g.tensor.matmul(T.pp[top, 0:HALF], T.vs[:], T.xs[:, top], start=True, stop=True).then_inc(sem.mm, 1)
    g.tensor.matmul(T.pp[bot, 0:HALF], T.vs[:], T.xs[:, bot], start=True, stop=True).then_inc(sem.mm, 1)
    g.vector.wait_ge(sem.mm, 2)
    g.vector.tensor_copy(T.ps[:], T.pp[:, 0:HALF]).then_inc(sem.pc, 1)

    g.wait_ge(sem.pc, 1)
    sent = 0
    off_chip = 0
    for j in near[rank]:
        off_chip |= topo.mask(core, cores[j])
    if relays[rank]:
        trs = []
        for k, (h, grp) in enumerate(relays[rank]):
            on_chip = topo.mask(core, h)
            stay = on_chip & ~off_chip
            trs.append(RemoteDMATransfer(dst_ids=[_dst(topo, h, core)],
                                         dma_engine_mask=_engines(stay, K_HAND, k * K_HAND),
                                         remote_sem=sem.h, src=T.ps[:], dst=T.ps[:]))
            sent += K_HAND
        g.remote_dma_fused(trs, local_sem=sem.ls)
    if near[rank]:
        slot = T.land[:, rank * HALF:(rank + 1) * HALF]
        g.remote_dma_fused(
            [RemoteDMATransfer(dst_ids=[_dst(topo, cores[j], core) for j in near[rank]],
                               dma_engine_mask=_engines(off_chip, K_NEAR),
                               remote_sem=sem["a%d" % rank], srcs=[T.ps[:]], dsts=[slot for j in near[rank]])],
            local_sem=sem.ls)
        sent += K_NEAR
    g.wait_ge(sem.ls, sent)

    g.vector.wait_ge(sem.lvt, 32)
    g.vector.tensor_tensor(T.vt2[:], T.vtt[:], T.vtt[:], AluOpType.add).then_inc(sem.nv, 1)

    far = [j for j in range(len(cores)) if j != rank and j not in near[rank]]
    order = [rank] + near[rank] + far
    g.tensor.wait_ge(sem.pc, 1)
    g.tensor.wait_ge(sem.nv, 1)
    for n, j in enumerate(order):
        if j == rank:
            piece = T.ps
            cols = slice(0, HALF)
        else:
            g.tensor.wait_ge(sem["a%d" % j], K_NEAR if j in near[rank] else K_FAR)
            piece = T.land
            cols = slice(j * HALF, (j + 1) * HALF)
        first, last = n == 0, n == len(order) - 1
        g.tensor.matmul(T.accl[:, 0:HALF], T.vt2[top, :], piece[top, cols], start=first, stop=last).then_inc(sem.fl, 1)
        g.tensor.matmul(T.accr[:, 0:HALF], T.vt2[bot, :], piece[bot, cols], start=first, stop=last).then_inc(sem.fr, 1)

    g.vector.wait_ge(sem.ld, 32)
    g.vector.wait_ge(sem.fl, len(order))
    g.vector.tensor_tensor(T.ys[:, top], T.xs[:, top], T.accl[:, 0:HALF], AluOpType.subtract).then_inc(sem.yd, 1)
    g.vector.wait_ge(sem.fr, len(order))
    g.vector.tensor_tensor(T.ys[:, bot], T.xs[:, bot], T.accr[:, 0:HALF], AluOpType.subtract).then_inc(sem.yd, 1)
    g.sync.wait_ge(sem.yd, 2)
    g.sync.dma_start(T.y[:], T.ys[:]).then_inc(sem.st, 16)
    g.sync.wait_ge(sem.st, 16)
